import numpy as np
import ml_dtypes


def mxq(x, axis, fmt="e4m3"):
    dtype, down = {"e4m3": (ml_dtypes.float8_e4m3fn, 7), "e5m2": (ml_dtypes.float8_e5m2, 14)}[fmt]
    v = np.moveaxis(np.asarray(x, np.float32).astype(ml_dtypes.bfloat16).astype(np.float64), axis, -1)
    blocks = v.reshape(v.shape[:-1] + (-1, 32))
    amax = np.abs(blocks).max(-1, keepdims=True)
    byte = np.maximum(np.where(amax > 0, np.frexp(amax)[1] - 1 + 127, 0) - down, 1)
    scale = np.exp2(byte - 127.0)
    codes = (blocks / scale).astype(np.float32).astype(dtype).astype(np.float64)
    return np.moveaxis((codes * scale).reshape(v.shape), -1, axis)


WIDE = False


def mx_kscale(k):
    if not WIDE:
        return np.ones(k)
    levels = np.array([10, -10, 5, -5, 0])
    if k % 512:
        return np.exp2(np.random.permutation(np.resize(levels, k // 32))).repeat(32)
    a = np.empty((k // 512, 16))
    for p in range(k // 512):
        a[p, :8] = np.random.permutation(np.resize(levels, 8))
        for g in range(8):
            far = levels[np.abs(levels - a[p, g]) >= 10]
            a[p, g + 8] = far[np.random.randint(len(far))]
    return np.exp2(a.ravel()).repeat(32)


def f64(x):
    return np.asarray(x).astype(np.float64)


def striped(idx):
    return np.tile(idx.reshape(-1, 16).T, (8, 1)).astype(np.uint16)


def unstriped(offs):
    return offs[:16].T.reshape(-1).astype(np.int64)


E2M1 = np.array([0.0, 0.5, 1.0, 1.5, 2.0, 3.0, 4.0, 6.0, -0.0, -0.5, -1.0, -1.5, -2.0, -3.0, -4.0, -6.0])


def pack_weight(w, fmt):
    k, n = w.shape
    w = f64(np.asarray(w, np.float32).astype(ml_dtypes.bfloat16)).reshape(k // 32, 32, n)
    amax = np.abs(w).max(1)
    if fmt == "e4m3":
        byte = np.frexp(amax)[1] - 1 + 127 - 7
    else:
        mant, ex = np.frexp(amax / 6.0)
        byte = np.where(mant > 0.5, ex, ex - 1) + 127
    byte = np.clip(np.where(amax > 0, byte, 1), 1, 254)
    scaled = (w * np.exp2(127.0 - byte)[:, None, :]).reshape(k, n).astype(np.float32)
    by_word = np.ascontiguousarray(scaled.reshape(k // 512, 128, 4, n).transpose(0, 1, 3, 2))
    if fmt == "e4m3":
        words = by_word.astype(ml_dtypes.float8_e4m3fn).view(np.uint8)
    else:
        c = by_word.astype(ml_dtypes.float4_e2m1fn).view(np.uint8) & 0xF
        words = (c[..., 0::2] | (c[..., 1::2] << 4)).reshape(k // 512, 128, 2 * n)
    return np.ascontiguousarray(words), np.ascontiguousarray(byte.astype(np.uint8).reshape(k // 512, 16, n))


def unpack_weight(words, scales, fmt):
    g, _, n = scales.shape
    words = np.ascontiguousarray(words).reshape(g, 128, n, -1)
    if fmt == "e4m3":
        vals = words.view(ml_dtypes.float8_e4m3fn).astype(np.float64)
    else:
        nib = np.empty((g, 128, n, 4), np.uint8)
        nib[..., 0::2] = words & 0xF
        nib[..., 1::2] = words >> 4
        vals = E2M1[nib]
    vals = vals * np.repeat(np.exp2(scales.astype(np.float64) - 127.0), 8, axis=1)[..., None]
    return vals.transpose(0, 1, 3, 2).reshape(g * 512, n)


def gelu(v):
    return 0.5 * v * (1.0 + np.tanh(np.sqrt(2.0 / np.pi) * (v + 0.044715 * v**3)))


K, H, N, T, S, P = 1024, 1024, 512, 2048, 1024, 512

def setup_inputs():
    n = np.random.standard_normal
    s = mx_kscale(K)[:, None]
    u = mx_kscale(H)[:, None]
    tab_words, tab_scales = pack_weight(n((K, T)) * s, "e4m3")
    w1 = 0.9 * n((K, H)) / np.sqrt(K) / s
    w2_words, w2_scales = pack_weight(2.0 * n((H, N)) / np.sqrt(H) / u, "e2m1")
    gain = P * np.random.uniform(0.6, 2.0, H) * u[:, 0]
    return {
        "tab_words": tab_words, "tab_scales": tab_scales,
        "offs": striped(np.random.permutation(T)[:S]),
        "pos1": striped(np.random.permutation(S)[:P]),
        "pos2": striped(np.random.permutation(S)[:P]),
        "w1": w1.astype(np.float32),
        "base": np.random.uniform(15.0, 90.0, H).astype(np.float32),
        "gain": gain.astype(np.float32),
        "w2_words": w2_words, "w2_scales": w2_scales,
    }

def reference(tab_words, tab_scales, offs, pos1, pos2, w1, base, gain, w2_words, w2_scales):
    v = unpack_weight(tab_words, tab_scales, "e4m3")[:, unstriped(offs)]
    h = mxq(f64(w1), 0, "e4m3").T @ v
    top = h.max(axis=1)
    a = np.exp(h[:, unstriped(pos1)] - top[:, None])
    c = h[:, unstriped(pos2)]
    share = a / (f64(base)[:, None] + a.sum(axis=1)[:, None])
    z = f64(gain)[:, None] * share * c
    w2 = unpack_weight(w2_words, w2_scales, "e2m1")
    y = w2.T @ mxq(z, 0, "e4m3")
    return np.log(1.0 + np.exp(y))

@@ -1,0 +1,270 @@
+from contextlib import ExitStack
+
+import concourse.mybir as mybir
+
+K, H, N, T, S, PL = 1024, 1024, 512, 2048, 1024, 512
+FLOPS = 2 * K * H * S + 2 * H * N * PL
+
+F32 = mybir.dt.float32
+BF16 = mybir.dt.bfloat16
+I32 = mybir.dt.int32
+U32 = mybir.dt.uint32
+U16 = mybir.dt.uint16
+U8 = mybir.dt.uint8
+FP8X4 = mybir.dt.float8_e4m3fn_x4
+FP4X4 = mybir.dt.float4_e2m1fn_x4
+ACT = mybir.ActivationFunctionType
+ALU = mybir.AluOpType
+
+P = 128
+BANK = 512
+HALF = 256
+EXP_CAP = 2.0**60
+LOOK_ACC = False
+
+
+def tile_list_platelet_urgency_kernel(
+    tc, tab_words, tab_scales, offs, pos1, pos2, w1, base, gain, w2_words, w2_scales, out
+):
+    nc = tc.nc
+    with ExitStack() as ctx:
+        keep = ctx.enter_context(tc.tile_pool(name="keep", bufs=1))
+        ring = ctx.enter_context(tc.tile_pool(name="ring", bufs=4))
+        psum_h = ctx.enter_context(tc.psum_pool(name="psum_h", bufs=2))
+        psum_y = ctx.enter_context(tc.psum_pool(name="psum_y", bufs=1))
+
+        def kept(name, shape, dtype):
+            return keep.tile(shape, dtype, name=name, align_bytes=64)
+
+        idx = kept("idx", [P, S // 16], U16)
+        p1 = kept("p1", [P, PL // 16], U16)
+        p2 = kept("p2", [P, PL // 16], U16)
+        tab_w = [kept("tab_w%d" % a, [P, T], U32) for a in range(2)]
+        tab_s = kept("tab_s", [P, T], U8)
+        v_w = [kept("v_w%d" % a, [P, S], U32) for a in range(2)]
+        v_s = kept("v_s", [P, S], U8)
+        w1_raw = {
+            (a, b, c): kept("w1_raw%d%d%d" % (a, b, c), [P, 4, HALF], F32)
+            for a in range(2) for b in range(2) for c in range(2)
+        }
+        w1_bf = {(a, b): kept("w1_bf%d%d" % (a, b), [P, 4 * BANK], BF16) for a in range(2) for b in range(2)}
+        w1_w = {(a, b): kept("w1_w%d%d" % (a, b), [P, BANK], U32) for a in range(2) for b in range(2)}
+        w1_s = {(a, b): kept("w1_s%d%d" % (a, b), [P, BANK], U8) for a in range(2) for b in range(2)}
+        w2_w = kept("w2_w", [P, 2, 2 * N], U8)
+        w2_s = kept("w2_s", [P, 2, N], U8)
+        base_t = kept("base_t", [P, 8], F32)
+        gain_t = kept("gain_t", [P, 8], F32)
+        base_share = kept("base_share", [P, 8], F32)
+        prod = [kept("prod%d" % i, [P, PL], F32) for i in range(8)]
+        den = [kept("den%d" % i, [P, 1], F32) for i in range(8)]
+        z_rows = [kept("z_rows%d" % b, [P, 4, PL], BF16) for b in range(2)]
+        z_bf = {(b, c): kept("z_bf%d%d" % (b, c), [P, HALF, 4], BF16) for b in range(2) for c in range(2)}
+        z_w = {(b, c): kept("z_w%d%d" % (b, c), [P, HALF], U32) for b in range(2) for c in range(2)}
+        z_s = {(b, c): kept("z_s%d%d" % (b, c), [P, HALF], U8) for b in range(2) for c in range(2)}
+        y_bank = {(c, g): psum_y.tile([P, 2, HALF], F32, name="y%d%d" % (c, g)) for c in range(2) for g in range(2)}
+        exp_y = kept("exp_y", [P, 4, BANK], F32)
+        one_plus = kept("one_plus", [P, 4, BANK], F32)
+
+        def load_w1(a, b, c):
+            cols = slice(BANK * b + HALF * c, BANK * b + HALF * (c + 1))
+            rows = w1[BANK * a : BANK * (a + 1), cols]
+            nc.sync.dma_start(out=w1_raw[a, b, c][:], in_=rows.rearrange("(p j) c -> p j c", j=4))
+
+        def load_tab(a):
+            nc.sync.dma_start(
+                out=tab_w[a][:].bitcast(I32),
+                in_=tab_words[a].rearrange("p t i -> p (t i)").bitcast(I32),
+            )
+
+        def round_w1(a, b, c, copy, m0=0, m1=64):
+            dst = w1_bf[a, b][:].rearrange("p (t m j) -> p m j t", t=4, j=4)
+            src = w1_raw[a, b, c][:].rearrange("p j (m t) -> p m j t", t=4)
+            copy(out=dst[:, 64 * c + m0 : 64 * c + m1], in_=src[:, m0:m1])
+
+        def quantize_w1(a, b, parts):
+            width = BANK // parts
+            for q in range(parts):
+                cols = slice(q * width, (q + 1) * width)
+                nc.vector.quantize_mx(
+                    out=w1_w[a, b][:, cols].bitcast(FP8X4),
+                    scales=w1_s[a, b][:, cols],
+                    in_=w1_bf[a, b][:, 4 * q * width : 4 * (q + 1) * width],
+                )
+
+        nc.vector.memset(tab_s[:].bitcast(I32), 0)
+        nc.vector.memset(w2_s[:].rearrange("p a n -> p (a n)").bitcast(I32), 0)
+        nc.sync.dma_start(out=idx[:], in_=offs)
+        for q in range(4):
+            nc.scalar.dma_start(
+                out=tab_s[32 * q : 32 * q + 8, :].bitcast(I32),
+                in_=tab_scales[:, 4 * q : 4 * q + 4, :].bitcast(I32),
+            )
+        load_tab(0)
+        load_w1(0, 0, 0)
+        load_w1(0, 0, 1)
+        load_tab(1)
+        load_w1(1, 0, 0)
+        load_w1(1, 0, 1)
+        nc.sync.dma_start(out=p1[:], in_=pos1)
+        nc.sync.dma_start(out=p2[:], in_=pos2)
+        nc.sync.dma_start(
+            out=base_t[:].rearrange("p (b t) -> p b t", t=4), in_=base.rearrange("(b p t) -> p b t", b=2, t=4)
+        )
+        nc.sync.dma_start(
+            out=gain_t[:].rearrange("p (b t) -> p b t", t=4), in_=gain.rearrange("(b p t) -> p b t", b=2, t=4)
+        )
+        for a in range(2):
+            for c in range(2):
+                load_w1(a, 1, c)
+        nc.sync.dma_start(out=w2_w[:].bitcast(I32), in_=w2_words.rearrange("a p c -> p a c").bitcast(I32))
+        for q in range(4):
+            nc.sync.dma_start(
+                out=w2_s[32 * q : 32 * q + 4].bitcast(I32),
+                in_=w2_scales[:, 4 * q : 4 * q + 4, :].rearrange("a r n -> r a n").bitcast(I32),
+            )
+
+        nc.vector.tensor_copy(out=v_s[:], in_=tab_s[:].indirect(idx[:]))
+        nc.vector.tensor_copy(out=v_w[0][:], in_=tab_w[0][:].indirect(idx[:]))
+        round_w1(0, 0, 0, nc.scalar.copy)
+        round_w1(0, 0, 1, nc.scalar.copy)
+        nc.vector.tensor_copy(out=v_w[1][:], in_=tab_w[1][:].indirect(idx[:]))
+        quantize_w1(0, 0, 1)
+        round_w1(1, 0, 0, nc.scalar.copy)
+        round_w1(1, 0, 1, nc.scalar.copy, 0, 24)
+        round_w1(1, 0, 1, nc.vector.tensor_copy, 24, 64)
+        quantize_w1(1, 0, 4)
+        nc.vector.tensor_scalar(out=base_share[:], in0=base_t[:], scalar1=1.0 / PL, scalar2=None, op0=ALU.mult)
+
+        h_rows, looked = {}, {}
+
+        def first_stage(i):
+            b, t = divmod(i, 4)
+            m_cols = slice(P * t, P * (t + 1))
+            h = ring.tile([P, S], F32, name="h")
+            tops = ring.tile([P, 2], F32, name="tops")
+            for half in range(2):
+                cols = slice(BANK * half, BANK * (half + 1))
+                acc = psum_h.tile([P, BANK], F32, name="acc%d" % half)
+                for a in range(2):
+                    nc.tensor.matmul_mx(
+                        out=acc[:],
+                        lhsT=w1_w[a, b][:, m_cols].bitcast(FP8X4),
+                        lhsT_scale=w1_s[a, b][:, m_cols],
+                        rhs=v_w[a][:, cols].bitcast(FP8X4),
+                        rhs_scale=v_s[4 * a :, cols],
+                        start=(a == 0),
+                        stop=(a == 1),
+                    )
+                nc.vector.tensor_scalar(
+                    out=h[:, cols], in0=acc[:], scalar1=1.0, scalar2=None, op0=ALU.mult, op1=ALU.max,
+                    accum_out=tops[:, half : half + 1],
+                )
+            neg_top = ring.tile([P, 1], F32, name="neg_top")
+            nc.vector.tensor_scalar(
+                out=neg_top[:], in0=tops[:, 0:1], scalar1=tops[:, 1:2], scalar2=-1.0, op0=ALU.max, op1=ALU.mult
+            )
+            a_look = ring.tile([P, PL], F32, name="a_look")
+            if LOOK_ACC:
+                nc.scalar.activation(
+                    out=a_look[:], in_=h[:].indirect(p1[:]), func=ACT.Exp, bias=neg_top[:], accum_out=den[i][:]
+                )
+            else:
+                nc.scalar.activation(out=a_look[:], in_=h[:].indirect(p1[:]), func=ACT.Exp, bias=neg_top[:])
+                shifted = ring.tile([P, PL], F32, name="shifted")
+                nc.scalar.activation(
+                    out=shifted[:], in_=a_look[:], func=ACT.Identity, bias=base_share[:, i : i + 1],
+                    accum_out=den[i][:],
+                )
+            h_rows[i], looked[i] = h, a_look
+
+        def pick(i):
+            nc.vector.tensor_tensor(out=prod[i][:], in0=h_rows[i][:].indirect(p2[:]), in1=looked[i][:], op=ALU.mult)
+
+        def scale_rows(i, on_vector):
+            b, t = divmod(i, 4)
+            inv = ring.tile([P, 1], F32, name="inv")
+            if LOOK_ACC:
+                full = ring.tile([P, 1], F32, name="full")
+                nc.vector.tensor_tensor(out=full[:], in0=den[i][:], in1=base_t[:, i : i + 1], op=ALU.add)
+                nc.vector.reciprocal(out=inv[:], in_=full[:])
+            else:
+                nc.vector.reciprocal(out=inv[:], in_=den[i][:])
+            if on_vector:
+                nc.vector.tensor_scalar(
+                    out=z_rows[b][:, t, :], in0=prod[i][:], scalar1=inv[:], scalar2=gain_t[:, i : i + 1],
+                    op0=ALU.mult, op1=ALU.mult,
+                )
+            else:
+                factor = ring.tile([P, 1], F32, name="factor")
+                nc.vector.tensor_tensor(out=factor[:], in0=inv[:], in1=gain_t[:, i : i + 1], op=ALU.mult)
+                nc.scalar.activation(out=z_rows[b][:, t, :], in_=prod[i][:], func=ACT.Copy, scale=factor[:])
+
+        def weave_z(b, c, copy):
+            src = z_rows[b][:, :, HALF * c : HALF * (c + 1)]
+            copy(
+                out=z_bf[b, c][:].rearrange("p (g i) t -> p g t i", i=4),
+                in_=src.rearrange("p t (g i) -> p g t i", i=4),
+            )
+
+        def second_stage(b, c):
+            nc.vector.quantize_mx(
+                out=z_w[b, c][:].bitcast(FP8X4), scales=z_s[b, c][:], in_=z_bf[b, c][:].rearrange("p m t -> p (m t)")
+            )
+            for g in range(2):
+                for j in range(2):
+                    n0 = P * (2 * g + j)
+                    nc.tensor.matmul_mx(
+                        out=y_bank[c, g][:, j, :],
+                        lhsT=w2_w[:, b, 2 * n0 : 2 * (n0 + P)].bitcast(FP4X4),
+                        lhsT_scale=w2_s[:, b, n0 : n0 + P],
+                        rhs=z_w[b, c][:].bitcast(FP8X4),
+                        rhs_scale=z_s[b, c][:],
+                        start=(b == 0 and j == 0),
+                        stop=(b == 1 and j == 1),
+                    )
+
+        first_stage(0)
+        round_w1(0, 1, 0, nc.scalar.copy)
+        first_stage(1)
+        round_w1(0, 1, 1, nc.scalar.copy)
+        for i in range(8):
+            if i + 2 < 8:
+                first_stage(i + 2)
+            pick(i)
+            scale_rows(i, on_vector=(i == 7))
+            if i == 0:
+                quantize_w1(0, 1, 1)
+                round_w1(1, 1, 0, nc.scalar.copy)
+                round_w1(1, 1, 1, nc.vector.tensor_copy)
+            if i == 1:
+                quantize_w1(1, 1, 1)
+            if i == 4:
+                weave_z(0, 0, nc.scalar.copy)
+                weave_z(0, 1, nc.scalar.copy)
+            if i == 6:
+                second_stage(0, 0)
+                second_stage(0, 1)
+        weave_z(1, 0, nc.vector.tensor_copy)
+        weave_z(1, 1, nc.scalar.copy)
+        second_stage(1, 0)
+        second_stage(1, 1)
+
+        banks = [(c, g) for c in range(2) for g in range(2)]
+        for k, key in enumerate(banks):
+            nc.scalar.activation(out=exp_y[:, k, :], in_=y_bank[key][:].rearrange("p j m -> p (j m)"), func=ACT.Exp)
+        nc.vector.tensor_scalar(
+            out=one_plus[:], in0=exp_y[:], scalar1=EXP_CAP, scalar2=1.0, op0=ALU.min, op1=ALU.add
+        )
+        pieces = [(k, 0, 2) for k in range(3)] + [(3, 0, 1), (3, 1, 2)]
+        for k, j0, j1 in pieces:
+            c, g = banks[k]
+            cols = slice(HALF * j0, HALF * j1)
+            log_t = keep.tile([P, HALF * (j1 - j0)], F32, name="log_t%d%d" % (k, j0))
+            nc.scalar.activation(out=log_t[:], in_=one_plus[:, k, cols], func=ACT.Ln)
+            res = keep.tile([P, j1 - j0, HALF], F32, name="res%d%d" % (k, j0))
+            nc.vector.tensor_tensor(
+                out=res[:].rearrange("p j m -> p (j m)"), in0=log_t[:],
+                in1=y_bank[c, g][:].rearrange("p j m -> p (j m)")[:, cols], op=ALU.max,
+            )
+            rows = out[P * (2 * g + j0) : P * (2 * g + j1), HALF * c : HALF * (c + 1)]
+            nc.sync.dma_start(out=rows.rearrange("(j p) m -> p j m", p=P), in_=res[:])

@@ -20,7 +20,6 @@ P = 128
 BANK = 512
 HALF = 256
 EXP_CAP = 2.0**60
-LOOK_ACC = False
 
 
 def tile_list_platelet_urgency_kernel(
@@ -29,7 +28,7 @@ def tile_list_platelet_urgency_kernel(
     nc = tc.nc
     with ExitStack() as ctx:
         keep = ctx.enter_context(tc.tile_pool(name="keep", bufs=1))
-        ring = ctx.enter_context(tc.tile_pool(name="ring", bufs=4))
+        ring = ctx.enter_context(tc.tile_pool(name="ring", bufs=5))
         psum_h = ctx.enter_context(tc.psum_pool(name="psum_h", bufs=2))
         psum_y = ctx.enter_context(tc.psum_pool(name="psum_y", bufs=1))
 
@@ -43,10 +42,8 @@ def tile_list_platelet_urgency_kernel(
         tab_s = kept("tab_s", [P, T], U8)
         v_w = [kept("v_w%d" % a, [P, S], U32) for a in range(2)]
         v_s = kept("v_s", [P, S], U8)
-        w1_raw = {
-            (a, b, c): kept("w1_raw%d%d%d" % (a, b, c), [P, 4, HALF], F32)
-            for a in range(2) for b in range(2) for c in range(2)
-        }
+        w1_raw = {(a, b): kept("w1_raw%d%d" % (a, b), [P, 4, BANK], F32) for a, b in ((0, 0), (0, 1), (1, 1))}
+        w1_last = [kept("w1_last%d" % c, [P, 4, HALF], F32) for c in range(2)]
         w1_bf = {(a, b): kept("w1_bf%d%d" % (a, b), [P, 4 * BANK], BF16) for a in range(2) for b in range(2)}
         w1_w = {(a, b): kept("w1_w%d%d" % (a, b), [P, BANK], U32) for a in range(2) for b in range(2)}
         w1_s = {(a, b): kept("w1_s%d%d" % (a, b), [P, BANK], U8) for a in range(2) for b in range(2)}
@@ -65,10 +62,9 @@ def tile_list_platelet_urgency_kernel(
         exp_y = kept("exp_y", [P, 4, BANK], F32)
         one_plus = kept("one_plus", [P, 4, BANK], F32)
 
-        def load_w1(a, b, c):
-            cols = slice(BANK * b + HALF * c, BANK * b + HALF * (c + 1))
-            rows = w1[BANK * a : BANK * (a + 1), cols]
-            nc.sync.dma_start(out=w1_raw[a, b, c][:], in_=rows.rearrange("(p j) c -> p j c", j=4))
+        def load_w1(dst, a, col0):
+            rows = w1[BANK * a : BANK * (a + 1), col0 : col0 + dst.shape[2]]
+            nc.sync.dma_start(out=dst[:], in_=rows.rearrange("(p j) c -> p j c", j=4))
 
         def load_tab(a):
             nc.sync.dma_start(
@@ -76,10 +72,10 @@ def tile_list_platelet_urgency_kernel(
                 in_=tab_words[a].rearrange("p t i -> p (t i)").bitcast(I32),
             )
 
-        def round_w1(a, b, c, copy, m0=0, m1=64):
+        def round_w1(a, b, raw, m_raw, m0, m1, copy):
             dst = w1_bf[a, b][:].rearrange("p (t m j) -> p m j t", t=4, j=4)
-            src = w1_raw[a, b, c][:].rearrange("p j (m t) -> p m j t", t=4)
-            copy(out=dst[:, 64 * c + m0 : 64 * c + m1], in_=src[:, m0:m1])
+            src = raw[:].rearrange("p j (m t) -> p m j t", t=4)
+            copy(out=dst[:, m0:m1], in_=src[:, m0 - m_raw : m1 - m_raw])
 
         def quantize_w1(a, b, parts):
             width = BANK // parts
@@ -92,30 +88,28 @@ def tile_list_platelet_urgency_kernel(
                 )
 
         nc.vector.memset(tab_s[:].bitcast(I32), 0)
-        nc.vector.memset(w2_s[:].rearrange("p a n -> p (a n)").bitcast(I32), 0)
+        nc.gpsimd.memset(w2_s[:].rearrange("p a n -> p (a n)").bitcast(I32), 0)
         nc.sync.dma_start(out=idx[:], in_=offs)
+        nc.sync.dma_start(out=p1[:], in_=pos1)
+        nc.sync.dma_start(out=p2[:], in_=pos2)
+        nc.scalar.dma_start(
+            out=base_t[:].rearrange("p (b t) -> p b t", t=4), in_=base.rearrange("(b p t) -> p b t", b=2, t=4)
+        )
+        nc.scalar.dma_start(
+            out=gain_t[:].rearrange("p (b t) -> p b t", t=4), in_=gain.rearrange("(b p t) -> p b t", b=2, t=4)
+        )
         for q in range(4):
             nc.scalar.dma_start(
                 out=tab_s[32 * q : 32 * q + 8, :].bitcast(I32),
                 in_=tab_scales[:, 4 * q : 4 * q + 4, :].bitcast(I32),
             )
         load_tab(0)
-        load_w1(0, 0, 0)
-        load_w1(0, 0, 1)
+        load_w1(w1_raw[0, 0], 0, 0)
         load_tab(1)
-        load_w1(1, 0, 0)
-        load_w1(1, 0, 1)
-        nc.sync.dma_start(out=p1[:], in_=pos1)
-        nc.sync.dma_start(out=p2[:], in_=pos2)
-        nc.sync.dma_start(
-            out=base_t[:].rearrange("p (b t) -> p b t", t=4), in_=base.rearrange("(b p t) -> p b t", b=2, t=4)
-        )
-        nc.sync.dma_start(
-            out=gain_t[:].rearrange("p (b t) -> p b t", t=4), in_=gain.rearrange("(b p t) -> p b t", b=2, t=4)
-        )
+        load_w1(w1_last[0], 1, 0)
+        load_w1(w1_last[1], 1, HALF)
         for a in range(2):
-            for c in range(2):
-                load_w1(a, 1, c)
+            load_w1(w1_raw[a, 1], a, BANK)
         nc.sync.dma_start(out=w2_w[:].bitcast(I32), in_=w2_words.rearrange("a p c -> p a c").bitcast(I32))
         for q in range(4):
             nc.sync.dma_start(
@@ -123,25 +117,27 @@ def tile_list_platelet_urgency_kernel(
                 in_=w2_scales[:, 4 * q : 4 * q + 4, :].rearrange("a r n -> r a n").bitcast(I32),
             )
 
-        nc.vector.tensor_copy(out=v_s[:], in_=tab_s[:].indirect(idx[:]))
         nc.vector.tensor_copy(out=v_w[0][:], in_=tab_w[0][:].indirect(idx[:]))
-        round_w1(0, 0, 0, nc.scalar.copy)
-        round_w1(0, 0, 1, nc.scalar.copy)
+        nc.vector.tensor_copy(out=v_s[:], in_=tab_s[:].indirect(idx[:]))
+        round_w1(0, 0, w1_raw[0, 0], 0, 0, 128, nc.scalar.copy)
         nc.vector.tensor_copy(out=v_w[1][:], in_=tab_w[1][:].indirect(idx[:]))
         quantize_w1(0, 0, 1)
-        round_w1(1, 0, 0, nc.scalar.copy)
-        round_w1(1, 0, 1, nc.scalar.copy, 0, 24)
-        round_w1(1, 0, 1, nc.vector.tensor_copy, 24, 64)
+        round_w1(1, 0, w1_last[0], 0, 0, 64, nc.scalar.copy)
+        round_w1(1, 0, w1_last[1], 64, 64, 96, nc.scalar.copy)
+        round_w1(1, 0, w1_last[1], 64, 96, 128, nc.vector.tensor_copy)
         quantize_w1(1, 0, 4)
-        nc.vector.tensor_scalar(out=base_share[:], in0=base_t[:], scalar1=1.0 / PL, scalar2=None, op0=ALU.mult)
+        nc.gpsimd.tensor_scalar(out=base_share[:], in0=base_t[:], scalar1=1.0 / PL, scalar2=0.0, op0=ALU.mult, op1=ALU.add)
 
-        h_rows, looked = {}, {}
+        h_rows, looked, neg_tops = {}, {}, {}
+        tops_of = {e: kept("tops%d" % e, [P, 2], F32) for e in range(3)}
+        for e, i in ((3, 0), (4, 2), (5, 3), (6, 4), (7, 5)):
+            tops_of[e] = prod[i]
 
         def first_stage(i):
             b, t = divmod(i, 4)
             m_cols = slice(P * t, P * (t + 1))
             h = ring.tile([P, S], F32, name="h")
-            tops = ring.tile([P, 2], F32, name="tops")
+            tops = tops_of[i]
             for half in range(2):
                 cols = slice(BANK * half, BANK * (half + 1))
                 acc = psum_h.tile([P, BANK], F32, name="acc%d" % half)
@@ -163,41 +159,38 @@ def tile_list_platelet_urgency_kernel(
             nc.vector.tensor_scalar(
                 out=neg_top[:], in0=tops[:, 0:1], scalar1=tops[:, 1:2], scalar2=-1.0, op0=ALU.max, op1=ALU.mult
             )
+            h_rows[i], neg_tops[i] = h, neg_top
+
+        def look(i):
+            h, neg_top = h_rows[i], neg_tops[i]
             a_look = ring.tile([P, PL], F32, name="a_look")
-            if LOOK_ACC:
-                nc.scalar.activation(
-                    out=a_look[:], in_=h[:].indirect(p1[:]), func=ACT.Exp, bias=neg_top[:], accum_out=den[i][:]
-                )
-            else:
-                nc.scalar.activation(out=a_look[:], in_=h[:].indirect(p1[:]), func=ACT.Exp, bias=neg_top[:])
-                shifted = ring.tile([P, PL], F32, name="shifted")
-                nc.scalar.activation(
-                    out=shifted[:], in_=a_look[:], func=ACT.Identity, bias=base_share[:, i : i + 1],
-                    accum_out=den[i][:],
-                )
-            h_rows[i], looked[i] = h, a_look
+            nc.scalar.activation(out=a_look[:], in_=h[:].indirect(p1[:]), func=ACT.Exp, bias=neg_top[:])
+            shifted = ring.tile([P, PL], F32, name="shifted")
+            nc.scalar.activation(
+                out=shifted[:], in_=a_look[:], func=ACT.Identity, bias=base_share[:, i : i + 1], accum_out=den[i][:]
+            )
+            looked[i] = a_look
 
         def pick(i):
             nc.vector.tensor_tensor(out=prod[i][:], in0=h_rows[i][:].indirect(p2[:]), in1=looked[i][:], op=ALU.mult)
 
-        def scale_rows(i, on_vector):
-            b, t = divmod(i, 4)
+        def invert(i):
             inv = ring.tile([P, 1], F32, name="inv")
-            if LOOK_ACC:
-                full = ring.tile([P, 1], F32, name="full")
-                nc.vector.tensor_tensor(out=full[:], in0=den[i][:], in1=base_t[:, i : i + 1], op=ALU.add)
-                nc.vector.reciprocal(out=inv[:], in_=full[:])
-            else:
-                nc.vector.reciprocal(out=inv[:], in_=den[i][:])
-            if on_vector:
-                nc.vector.tensor_scalar(
-                    out=z_rows[b][:, t, :], in0=prod[i][:], scalar1=inv[:], scalar2=gain_t[:, i : i + 1],
-                    op0=ALU.mult, op1=ALU.mult,
-                )
-            else:
-                factor = ring.tile([P, 1], F32, name="factor")
-                nc.vector.tensor_tensor(out=factor[:], in0=inv[:], in1=gain_t[:, i : i + 1], op=ALU.mult)
-                nc.scalar.activation(out=z_rows[b][:, t, :], in_=prod[i][:], func=ACT.Copy, scale=factor[:])
+            nc.vector.reciprocal(out=inv[:], in_=den[i][:])
+            return inv
+
+        def scale_rows(i, inv, engine):
+            b, t = divmod(i, 4)
+            engine.tensor_scalar(
+                out=z_rows[b][:, t, :], in0=prod[i][:], scalar1=inv[:], scalar2=gain_t[:, i : i + 1],
+                op0=ALU.mult, op1=ALU.mult,
+            )
+
+        def scale_rows_on_scalar(i, inv):
+            b, t = divmod(i, 4)
+            factor = ring.tile([P, 1], F32, name="factor")
+            nc.vector.tensor_tensor(out=factor[:], in0=inv[:], in1=gain_t[:, i : i + 1], op=ALU.mult)
+            nc.scalar.activation(out=z_rows[b][:, t, :], in_=prod[i][:], func=ACT.Copy, scale=factor[:])
 
         def weave_z(b, c, copy):
             src = z_rows[b][:, :, HALF * c : HALF * (c + 1)]
@@ -224,26 +217,42 @@ def tile_list_platelet_urgency_kernel(
                     )
 
         first_stage(0)
-        round_w1(0, 1, 0, nc.scalar.copy)
+        round_w1(0, 1, w1_raw[0, 1], 0, 0, 64, nc.scalar.copy)
+        round_w1(0, 1, w1_raw[0, 1], 0, 64, 128, nc.scalar.copy)
+        look(0)
         first_stage(1)
-        round_w1(0, 1, 1, nc.scalar.copy)
-        for i in range(8):
-            if i + 2 < 8:
-                first_stage(i + 2)
-            pick(i)
-            scale_rows(i, on_vector=(i == 7))
-            if i == 0:
-                quantize_w1(0, 1, 1)
-                round_w1(1, 1, 0, nc.scalar.copy)
-                round_w1(1, 1, 1, nc.vector.tensor_copy)
-            if i == 1:
-                quantize_w1(1, 1, 1)
+        round_w1(1, 1, w1_raw[1, 1], 0, 0, 64, nc.scalar.copy)
+        round_w1(1, 1, w1_raw[1, 1], 0, 64, 128, nc.scalar.copy)
+        look(1)
+        first_stage(2)
+        look(2)
+        quantize_w1(0, 1, 1)
+        first_stage(3)
+        look(3)
+        pick(0)
+        quantize_w1(1, 1, 1)
+        pick(1)
+        scale_rows(0, invert(0), nc.gpsimd)
+        scale_rows(1, invert(1), nc.gpsimd)
+        for i in range(2, 5):
+            first_stage(i + 2)
             if i == 4:
                 weave_z(0, 0, nc.scalar.copy)
-                weave_z(0, 1, nc.scalar.copy)
-            if i == 6:
-                second_stage(0, 0)
-                second_stage(0, 1)
+            look(i + 2)
+            inv = invert(i)
+            pick(i)
+            scale_rows(i, inv, nc.gpsimd)
+        first_stage(7)
+        look(7)
+        weave_z(0, 1, nc.scalar.copy)
+        for i in range(5, 7):
+            inv = invert(i)
+            pick(i)
+            scale_rows_on_scalar(i, inv)
+            second_stage(0, i - 5)
+        inv = invert(7)
+        pick(7)
+        scale_rows(7, inv, nc.vector)
         weave_z(1, 0, nc.vector.tensor_copy)
         weave_z(1, 1, nc.scalar.copy)
         second_stage(1, 0)

@@ -29,8 +29,7 @@ def tile_list_platelet_urgency_kernel(
     with ExitStack() as ctx:
         keep = ctx.enter_context(tc.tile_pool(name="keep", bufs=1))
         ring = ctx.enter_context(tc.tile_pool(name="ring", bufs=5))
-        psum_h = ctx.enter_context(tc.psum_pool(name="psum_h", bufs=2))
-        psum_y = ctx.enter_context(tc.psum_pool(name="psum_y", bufs=1))
+        psum = ctx.enter_context(tc.psum_pool(name="psum", bufs=1))
 
         def kept(name, shape, dtype):
             return keep.tile(shape, dtype, name=name, align_bytes=64)
@@ -55,10 +54,10 @@ def tile_list_platelet_urgency_kernel(
         prod = [kept("prod%d" % i, [P, PL], F32) for i in range(8)]
         den = [kept("den%d" % i, [P, 1], F32) for i in range(8)]
         z_rows = [kept("z_rows%d" % b, [P, 4, PL], BF16) for b in range(2)]
-        z_bf = {(b, c): kept("z_bf%d%d" % (b, c), [P, HALF, 4], BF16) for b in range(2) for c in range(2)}
-        z_w = {(b, c): kept("z_w%d%d" % (b, c), [P, HALF], U32) for b in range(2) for c in range(2)}
-        z_s = {(b, c): kept("z_s%d%d" % (b, c), [P, HALF], U8) for b in range(2) for c in range(2)}
-        y_bank = {(c, g): psum_y.tile([P, 2, HALF], F32, name="y%d%d" % (c, g)) for c in range(2) for g in range(2)}
+        z_bf = {(b, c): kept("z_bf%d%d" % (b, c), [P, P, 4], BF16) for b in range(2) for c in range(4)}
+        z_w = {(b, c): kept("z_w%d%d" % (b, c), [P, P], U32) for b in range(2) for c in range(4)}
+        z_s = {(b, c): kept("z_s%d%d" % (b, c), [P, P], U8) for b in range(2) for c in range(4)}
+        y_bank = {}
         exp_y = kept("exp_y", [P, 4, BANK], F32)
         one_plus = kept("one_plus", [P, 4, BANK], F32)
 
@@ -72,9 +71,12 @@ def tile_list_platelet_urgency_kernel(
                 in_=tab_words[a].rearrange("p t i -> p (t i)").bitcast(I32),
             )
 
-        def round_w1(a, b, raw, m_raw, m0, m1, copy):
-            dst = w1_bf[a, b][:].rearrange("p (t m j) -> p m j t", t=4, j=4)
-            src = raw[:].rearrange("p j (m t) -> p m j t", t=4)
+        def copy_on_gpsimd(out, in_):
+            nc.gpsimd.tensor_scalar(out=out, in0=in_, scalar1=1.0, scalar2=0.0, op0=ALU.mult, op1=ALU.add)
+
+        def round_w1(a, b, raw, m_raw, m0, m1, copy, walk="p m t j"):
+            dst = w1_bf[a, b][:].rearrange("p (t m j) -> " + walk, t=4, j=4)
+            src = raw[:].rearrange("p j (m t) -> " + walk, t=4)
             copy(out=dst[:, m0:m1], in_=src[:, m0 - m_raw : m1 - m_raw])
 
         def quantize_w1(a, b, parts):
@@ -140,7 +142,7 @@ def tile_list_platelet_urgency_kernel(
             tops = tops_of[i]
             for half in range(2):
                 cols = slice(BANK * half, BANK * (half + 1))
-                acc = psum_h.tile([P, BANK], F32, name="acc%d" % half)
+                acc = psum.tile([P, BANK], F32, name="acc", tag="bank%d" % ((2 * i + half) % 8))
                 for a in range(2):
                     nc.tensor.matmul_mx(
                         out=acc[:],
@@ -193,7 +195,7 @@ def tile_list_platelet_urgency_kernel(
             nc.scalar.activation(out=z_rows[b][:, t, :], in_=prod[i][:], func=ACT.Copy, scale=factor[:])
 
         def weave_z(b, c, copy):
-            src = z_rows[b][:, :, HALF * c : HALF * (c + 1)]
+            src = z_rows[b][:, :, P * c : P * (c + 1)]
             copy(
                 out=z_bf[b, c][:].rearrange("p (g i) t -> p g t i", i=4),
                 in_=src.rearrange("p t (g i) -> p g t i", i=4),
@@ -203,77 +205,77 @@ def tile_list_platelet_urgency_kernel(
             nc.vector.quantize_mx(
                 out=z_w[b, c][:].bitcast(FP8X4), scales=z_s[b, c][:], in_=z_bf[b, c][:].rearrange("p m t -> p (m t)")
             )
-            for g in range(2):
-                for j in range(2):
-                    n0 = P * (2 * g + j)
-                    nc.tensor.matmul_mx(
-                        out=y_bank[c, g][:, j, :],
-                        lhsT=w2_w[:, b, 2 * n0 : 2 * (n0 + P)].bitcast(FP4X4),
-                        lhsT_scale=w2_s[:, b, n0 : n0 + P],
-                        rhs=z_w[b, c][:].bitcast(FP8X4),
-                        rhs_scale=z_s[b, c][:],
-                        start=(b == 0 and j == 0),
-                        stop=(b == 1 and j == 1),
-                    )
+            if b == 0:
+                y_bank[c] = psum.tile([P, BANK], F32, name="y", tag="bank%d" % c)
+            for j in range(4):
+                n0 = P * j
+                nc.tensor.matmul_mx(
+                    out=y_bank[c][:, n0 : n0 + P],
+                    lhsT=w2_w[:, b, 2 * n0 : 2 * (n0 + P)].bitcast(FP4X4),
+                    lhsT_scale=w2_s[:, b, n0 : n0 + P],
+                    rhs=z_w[b, c][:].bitcast(FP8X4),
+                    rhs_scale=z_s[b, c][:],
+                    start=(b == 0 and j == 0),
+                    stop=(b == 1 and j == 3),
+                )
 
         first_stage(0)
         round_w1(0, 1, w1_raw[0, 1], 0, 0, 64, nc.scalar.copy)
-        round_w1(0, 1, w1_raw[0, 1], 0, 64, 128, nc.scalar.copy)
+        round_w1(0, 1, w1_raw[0, 1], 0, 64, 128, copy_on_gpsimd)
         look(0)
         first_stage(1)
-        round_w1(1, 1, w1_raw[1, 1], 0, 0, 64, nc.scalar.copy)
-        round_w1(1, 1, w1_raw[1, 1], 0, 64, 128, nc.scalar.copy)
+        round_w1(1, 1, w1_raw[1, 1], 0, 0, 40, copy_on_gpsimd)
+        round_w1(1, 1, w1_raw[1, 1], 0, 40, 80, copy_on_gpsimd)
+        round_w1(1, 1, w1_raw[1, 1], 0, 80, 128, nc.scalar.copy)
         look(1)
         first_stage(2)
         look(2)
-        quantize_w1(0, 1, 1)
         first_stage(3)
         look(3)
-        pick(0)
+        quantize_w1(0, 1, 1)
         quantize_w1(1, 1, 1)
-        pick(1)
-        scale_rows(0, invert(0), nc.gpsimd)
-        scale_rows(1, invert(1), nc.gpsimd)
-        for i in range(2, 5):
-            first_stage(i + 2)
-            if i == 4:
-                weave_z(0, 0, nc.scalar.copy)
-            look(i + 2)
+        inv = invert(0)
+        pick(0)
+        scale_rows_on_scalar(0, inv)
+        for i in range(1, 5):
             inv = invert(i)
             pick(i)
             scale_rows(i, inv, nc.gpsimd)
-        first_stage(7)
-        look(7)
-        weave_z(0, 1, nc.scalar.copy)
+            first_stage(i + 3)
+            if i == 3:
+                weave_z(0, 0, nc.scalar.copy)
+                weave_z(0, 1, nc.scalar.copy)
+            look(i + 3)
+        weave_z(0, 2, nc.scalar.copy)
+        weave_z(0, 3, nc.scalar.copy)
         for i in range(5, 7):
             inv = invert(i)
             pick(i)
             scale_rows_on_scalar(i, inv)
-            second_stage(0, i - 5)
+            second_stage(0, 2 * (i - 5))
+            second_stage(0, 2 * (i - 5) + 1)
         inv = invert(7)
         pick(7)
         scale_rows(7, inv, nc.vector)
         weave_z(1, 0, nc.vector.tensor_copy)
-        weave_z(1, 1, nc.scalar.copy)
-        second_stage(1, 0)
-        second_stage(1, 1)
+        for c in range(4):
+            if c + 1 < 4:
+                weave_z(1, c + 1, nc.vector.tensor_copy)
+            second_stage(1, c)
 
-        banks = [(c, g) for c in range(2) for g in range(2)]
-        for k, key in enumerate(banks):
-            nc.scalar.activation(out=exp_y[:, k, :], in_=y_bank[key][:].rearrange("p j m -> p (j m)"), func=ACT.Exp)
+        for c in range(4):
+            nc.scalar.activation(out=exp_y[:, c, :], in_=y_bank[c][:], func=ACT.Exp)
         nc.vector.tensor_scalar(
             out=one_plus[:], in0=exp_y[:], scalar1=EXP_CAP, scalar2=1.0, op0=ALU.min, op1=ALU.add
         )
-        pieces = [(k, 0, 2) for k in range(3)] + [(3, 0, 1), (3, 1, 2)]
-        for k, j0, j1 in pieces:
-            c, g = banks[k]
-            cols = slice(HALF * j0, HALF * j1)
-            log_t = keep.tile([P, HALF * (j1 - j0)], F32, name="log_t%d%d" % (k, j0))
-            nc.scalar.activation(out=log_t[:], in_=one_plus[:, k, cols], func=ACT.Ln)
-            res = keep.tile([P, j1 - j0, HALF], F32, name="res%d%d" % (k, j0))
+        pieces = [(0, 0, 2), (0, 2, 4), (1, 0, 4), (2, 0, 4), (3, 0, 2), (3, 2, 4)]
+        for c, j0, j1 in pieces:
+            cols = slice(P * j0, P * j1)
+            log_t = keep.tile([P, P * (j1 - j0)], F32, name="log_t%d%d" % (c, j0))
+            nc.scalar.activation(out=log_t[:], in_=one_plus[:, c, cols], func=ACT.Ln)
+            res = keep.tile([P, j1 - j0, P], F32, name="res%d%d" % (c, j0))
             nc.vector.tensor_tensor(
-                out=res[:].rearrange("p j m -> p (j m)"), in0=log_t[:],
-                in1=y_bank[c, g][:].rearrange("p j m -> p (j m)")[:, cols], op=ALU.max,
+                out=res[:].rearrange("p j m -> p (j m)"), in0=log_t[:], in1=y_bank[c][:, cols], op=ALU.max
             )
-            rows = out[P * (2 * g + j0) : P * (2 * g + j1), HALF * c : HALF * (c + 1)]
+            rows = out[P * j0 : P * j1, P * c : P * (c + 1)]
             nc.sync.dma_start(out=rows.rearrange("(j p) m -> p j m", p=P), in_=res[:])

@@ -46,7 +46,7 @@ def tile_list_platelet_urgency_kernel(
         w1_bf = {(a, b): kept("w1_bf%d%d" % (a, b), [P, 4 * BANK], BF16) for a in range(2) for b in range(2)}
         w1_w = {(a, b): kept("w1_w%d%d" % (a, b), [P, BANK], U32) for a in range(2) for b in range(2)}
         w1_s = {(a, b): kept("w1_s%d%d" % (a, b), [P, BANK], U8) for a in range(2) for b in range(2)}
-        w2_w = kept("w2_w", [P, 2, 2 * N], U8)
+        w2_w = [kept("w2_w%d" % a, [P, 2 * N], U8) for a in range(2)]
         w2_s = kept("w2_s", [P, 2, N], U8)
         base_t = kept("base_t", [P, 8], F32)
         gain_t = kept("gain_t", [P, 8], F32)
@@ -94,12 +94,8 @@ def tile_list_platelet_urgency_kernel(
         nc.sync.dma_start(out=idx[:], in_=offs)
         nc.sync.dma_start(out=p1[:], in_=pos1)
         nc.sync.dma_start(out=p2[:], in_=pos2)
-        nc.scalar.dma_start(
-            out=base_t[:].rearrange("p (b t) -> p b t", t=4), in_=base.rearrange("(b p t) -> p b t", b=2, t=4)
-        )
-        nc.scalar.dma_start(
-            out=gain_t[:].rearrange("p (b t) -> p b t", t=4), in_=gain.rearrange("(b p t) -> p b t", b=2, t=4)
-        )
+        for a in range(2):
+            nc.scalar.dma_start(out=w2_w[a][:].bitcast(I32), in_=w2_words[a].bitcast(I32))
         for q in range(4):
             nc.scalar.dma_start(
                 out=tab_s[32 * q : 32 * q + 8, :].bitcast(I32),
@@ -112,7 +108,12 @@ def tile_list_platelet_urgency_kernel(
         load_w1(w1_last[1], 1, HALF)
         for a in range(2):
             load_w1(w1_raw[a, 1], a, BANK)
-        nc.sync.dma_start(out=w2_w[:].bitcast(I32), in_=w2_words.rearrange("a p c -> p a c").bitcast(I32))
+        nc.sync.dma_start(
+            out=base_t[:].rearrange("p (b t) -> p b t", t=4), in_=base.rearrange("(b p t) -> p b t", b=2, t=4)
+        )
+        nc.sync.dma_start(
+            out=gain_t[:].rearrange("p (b t) -> p b t", t=4), in_=gain.rearrange("(b p t) -> p b t", b=2, t=4)
+        )
         for q in range(4):
             nc.sync.dma_start(
                 out=w2_s[32 * q : 32 * q + 4].bitcast(I32),
@@ -131,15 +132,13 @@ def tile_list_platelet_urgency_kernel(
         nc.gpsimd.tensor_scalar(out=base_share[:], in0=base_t[:], scalar1=1.0 / PL, scalar2=0.0, op0=ALU.mult, op1=ALU.add)
 
         h_rows, looked, neg_tops = {}, {}, {}
-        tops_of = {e: kept("tops%d" % e, [P, 2], F32) for e in range(3)}
-        for e, i in ((3, 0), (4, 2), (5, 3), (6, 4), (7, 5)):
-            tops_of[e] = prod[i]
+        tops_of = {}
 
         def first_stage(i):
             b, t = divmod(i, 4)
             m_cols = slice(P * t, P * (t + 1))
             h = ring.tile([P, S], F32, name="h")
-            tops = tops_of[i]
+            tops = ring.tile([P, 2], F32, name="tops")
             for half in range(2):
                 cols = slice(BANK * half, BANK * (half + 1))
                 acc = psum.tile([P, BANK], F32, name="acc", tag="bank%d" % ((2 * i + half) % 8))
@@ -157,41 +156,54 @@ def tile_list_platelet_urgency_kernel(
                     out=h[:, cols], in0=acc[:], scalar1=1.0, scalar2=None, op0=ALU.mult, op1=ALU.max,
                     accum_out=tops[:, half : half + 1],
                 )
+            h_rows[i], tops_of[i] = h, tops
+
+        def negate_top(i):
+            tops = tops_of[i]
             neg_top = ring.tile([P, 1], F32, name="neg_top")
             nc.vector.tensor_scalar(
                 out=neg_top[:], in0=tops[:, 0:1], scalar1=tops[:, 1:2], scalar2=-1.0, op0=ALU.max, op1=ALU.mult
             )
-            h_rows[i], neg_tops[i] = h, neg_top
+            neg_tops[i] = neg_top
 
         def look(i):
             h, neg_top = h_rows[i], neg_tops[i]
             a_look = ring.tile([P, PL], F32, name="a_look")
             nc.scalar.activation(out=a_look[:], in_=h[:].indirect(p1[:]), func=ACT.Exp, bias=neg_top[:])
+            looked[i] = a_look
+
+        def row_sum(i):
+            a_look = looked[i]
             shifted = ring.tile([P, PL], F32, name="shifted")
             nc.scalar.activation(
                 out=shifted[:], in_=a_look[:], func=ACT.Identity, bias=base_share[:, i : i + 1], accum_out=den[i][:]
             )
-            looked[i] = a_look
 
-        def pick(i):
-            nc.vector.tensor_tensor(out=prod[i][:], in0=h_rows[i][:].indirect(p2[:]), in1=looked[i][:], op=ALU.mult)
+        def pick(i, m0=0, m1=PL):
+            nc.vector.tensor_tensor(
+                out=prod[i][:, m0:m1], in0=h_rows[i][:].indirect(p2[:, m0 // 16 : m1 // 16]),
+                in1=looked[i][:, m0:m1], op=ALU.mult,
+            )
 
         def invert(i):
             inv = ring.tile([P, 1], F32, name="inv")
             nc.vector.reciprocal(out=inv[:], in_=den[i][:])
             return inv
 
-        def scale_rows(i, inv, engine):
+        def times_gain(i, inv):
+            factor = ring.tile([P, 1], F32, name="factor")
+            nc.vector.tensor_tensor(out=factor[:], in0=inv[:], in1=gain_t[:, i : i + 1], op=ALU.mult)
+            return factor
+
+        def scale_rows(i, inv, engine, m0=0, m1=PL):
             b, t = divmod(i, 4)
             engine.tensor_scalar(
-                out=z_rows[b][:, t, :], in0=prod[i][:], scalar1=inv[:], scalar2=gain_t[:, i : i + 1],
+                out=z_rows[b][:, t, m0:m1], in0=prod[i][:, m0:m1], scalar1=inv[:], scalar2=gain_t[:, i : i + 1],
                 op0=ALU.mult, op1=ALU.mult,
             )
 
-        def scale_rows_on_scalar(i, inv):
+        def scale_rows_on_scalar(i, factor):
             b, t = divmod(i, 4)
-            factor = ring.tile([P, 1], F32, name="factor")
-            nc.vector.tensor_tensor(out=factor[:], in0=inv[:], in1=gain_t[:, i : i + 1], op=ALU.mult)
             nc.scalar.activation(out=z_rows[b][:, t, :], in_=prod[i][:], func=ACT.Copy, scale=factor[:])
 
         def weave_z(b, c, copy):
@@ -211,7 +223,7 @@ def tile_list_platelet_urgency_kernel(
                 n0 = P * j
                 nc.tensor.matmul_mx(
                     out=y_bank[c][:, n0 : n0 + P],
-                    lhsT=w2_w[:, b, 2 * n0 : 2 * (n0 + P)].bitcast(FP4X4),
+                    lhsT=w2_w[b][:, 2 * n0 : 2 * (n0 + P)].bitcast(FP4X4),
                     lhsT_scale=w2_s[:, b, n0 : n0 + P],
                     rhs=z_w[b, c][:].bitcast(FP8X4),
                     rhs_scale=z_s[b, c][:],
@@ -222,46 +234,72 @@ def tile_list_platelet_urgency_kernel(
         first_stage(0)
         round_w1(0, 1, w1_raw[0, 1], 0, 0, 64, nc.scalar.copy)
         round_w1(0, 1, w1_raw[0, 1], 0, 64, 128, copy_on_gpsimd)
-        look(0)
         first_stage(1)
+        negate_top(0)
+        look(0)
         round_w1(1, 1, w1_raw[1, 1], 0, 0, 40, copy_on_gpsimd)
         round_w1(1, 1, w1_raw[1, 1], 0, 40, 80, copy_on_gpsimd)
         round_w1(1, 1, w1_raw[1, 1], 0, 80, 128, nc.scalar.copy)
-        look(1)
+        row_sum(0)
         first_stage(2)
-        look(2)
+        negate_top(1)
+        look(1)
+        row_sum(1)
         first_stage(3)
-        look(3)
+        negate_top(2)
+        look(2)
+        row_sum(2)
         quantize_w1(0, 1, 1)
-        quantize_w1(1, 1, 1)
+        negate_top(3)
+        look(3)
+        row_sum(3)
         inv = invert(0)
+        quantize_w1(1, 1, 1)
+        factor = times_gain(0, inv)
         pick(0)
-        scale_rows_on_scalar(0, inv)
-        for i in range(1, 5):
+        scale_rows_on_scalar(0, factor)
+        inv = invert(1)
+        pick(1)
+        scale_rows(1, inv, nc.gpsimd)
+        for i in range(2, 5):
+            first_stage(i + 2)
             inv = invert(i)
             pick(i)
             scale_rows(i, inv, nc.gpsimd)
-            first_stage(i + 3)
-            if i == 3:
+            negate_top(i + 2)
+            if i == 4:
                 weave_z(0, 0, nc.scalar.copy)
                 weave_z(0, 1, nc.scalar.copy)
-            look(i + 3)
+            look(i + 2)
+            row_sum(i + 2)
+        first_stage(7)
+        inv = invert(5)
+        negate_top(7)
+        look(7)
+        row_sum(7)
+        factor = times_gain(5, inv)
+        pick(5)
+        scale_rows_on_scalar(5, factor)
+        inv = invert(6)
+        second_stage(0, 0)
+        factor = times_gain(6, inv)
+        pick(6)
+        scale_rows_on_scalar(6, factor)
         weave_z(0, 2, nc.scalar.copy)
         weave_z(0, 3, nc.scalar.copy)
-        for i in range(5, 7):
-            inv = invert(i)
-            pick(i)
-            scale_rows_on_scalar(i, inv)
-            second_stage(0, 2 * (i - 5))
-            second_stage(0, 2 * (i - 5) + 1)
+        second_stage(0, 1)
         inv = invert(7)
-        pick(7)
-        scale_rows(7, inv, nc.vector)
+        pick(7, 0, HALF)
+        pick(7, HALF, PL)
+        scale_rows(7, inv, nc.vector, 0, HALF)
+        scale_rows(7, inv, nc.vector, HALF, PL)
         weave_z(1, 0, nc.vector.tensor_copy)
         for c in range(4):
             if c + 1 < 4:
                 weave_z(1, c + 1, nc.vector.tensor_copy)
             second_stage(1, c)
+            if c in (0, 1):
+                second_stage(0, c + 2)
 
         for c in range(4):
             nc.scalar.activation(out=exp_y[:, c, :], in_=y_bank[c][:], func=ACT.Exp)

from contextlib import ExitStack

import concourse.mybir as mybir

K, H, N, T, S, PL = 1024, 1024, 512, 2048, 1024, 512
FLOPS = 2 * K * H * S + 2 * H * N * PL

F32 = mybir.dt.float32
BF16 = mybir.dt.bfloat16
I32 = mybir.dt.int32
U32 = mybir.dt.uint32
U16 = mybir.dt.uint16
U8 = mybir.dt.uint8
FP8X4 = mybir.dt.float8_e4m3fn_x4
FP4X4 = mybir.dt.float4_e2m1fn_x4
ACT = mybir.ActivationFunctionType
ALU = mybir.AluOpType

P = 128
BANK = 512
HALF = 256
EXP_CAP = 2.0**60


def tile_list_platelet_urgency_kernel(
    tc, tab_words, tab_scales, offs, pos1, pos2, w1, base, gain, w2_words, w2_scales, out
):
    nc = tc.nc
    with ExitStack() as ctx:
        keep = ctx.enter_context(tc.tile_pool(name="keep", bufs=1))
        ring = ctx.enter_context(tc.tile_pool(name="ring", bufs=5))
        psum = ctx.enter_context(tc.psum_pool(name="psum", bufs=1))

        def kept(name, shape, dtype):
            return keep.tile(shape, dtype, name=name, align_bytes=64)

        idx = kept("idx", [P, S // 16], U16)
        p1 = kept("p1", [P, PL // 16], U16)
        p2 = kept("p2", [P, PL // 16], U16)
        tab_w = [kept("tab_w%d" % a, [P, T], U32) for a in range(2)]
        tab_s = kept("tab_s", [P, T], U8)
        v_w = [kept("v_w%d" % a, [P, S], U32) for a in range(2)]
        v_s = kept("v_s", [P, S], U8)
        w1_raw = {(a, b): kept("w1_raw%d%d" % (a, b), [P, 4, BANK], F32) for a, b in ((0, 0), (0, 1), (1, 1))}
        w1_last = [kept("w1_last%d" % c, [P, 4, HALF], F32) for c in range(2)]
        w1_bf = {(a, b): kept("w1_bf%d%d" % (a, b), [P, 4 * BANK], BF16) for a in range(2) for b in range(2)}
        w1_w = {(a, b): kept("w1_w%d%d" % (a, b), [P, BANK], U32) for a in range(2) for b in range(2)}
        w1_s = {(a, b): kept("w1_s%d%d" % (a, b), [P, BANK], U8) for a in range(2) for b in range(2)}
        w2_w = [kept("w2_w%d" % a, [P, 2 * N], U8) for a in range(2)]
        w2_s = kept("w2_s", [P, 2, N], U8)
        base_t = kept("base_t", [P, 8], F32)
        gain_t = kept("gain_t", [P, 8], F32)
        base_share = kept("base_share", [P, 8], F32)
        prod = [kept("prod%d" % i, [P, PL], F32) for i in range(8)]
        den = [kept("den%d" % i, [P, 1], F32) for i in range(8)]
        z_rows = [kept("z_rows%d" % b, [P, 4, PL], BF16) for b in range(2)]
        z_bf = {(b, c): kept("z_bf%d%d" % (b, c), [P, P, 4], BF16) for b in range(2) for c in range(4)}
        z_w = {(b, c): kept("z_w%d%d" % (b, c), [P, P], U32) for b in range(2) for c in range(4)}
        z_s = {(b, c): kept("z_s%d%d" % (b, c), [P, P], U8) for b in range(2) for c in range(4)}
        y_bank = {}
        exp_y = kept("exp_y", [P, 4, BANK], F32)
        one_plus = kept("one_plus", [P, 4, BANK], F32)

        def load_w1(dst, a, col0):
            rows = w1[BANK * a : BANK * (a + 1), col0 : col0 + dst.shape[2]]
            nc.sync.dma_start(out=dst[:], in_=rows.rearrange("(p j) c -> p j c", j=4))

        def load_tab(a):
            nc.sync.dma_start(
                out=tab_w[a][:].bitcast(I32),
                in_=tab_words[a].rearrange("p t i -> p (t i)").bitcast(I32),
            )

        def copy_on_gpsimd(out, in_):
            nc.gpsimd.tensor_scalar(out=out, in0=in_, scalar1=1.0, scalar2=0.0, op0=ALU.mult, op1=ALU.add)

        def round_w1(a, b, raw, m_raw, m0, m1, copy, walk="p m t j"):
            dst = w1_bf[a, b][:].rearrange("p (t m j) -> " + walk, t=4, j=4)
            src = raw[:].rearrange("p j (m t) -> " + walk, t=4)
            copy(out=dst[:, m0:m1], in_=src[:, m0 - m_raw : m1 - m_raw])

        def quantize_w1(a, b, parts):
            width = BANK // parts
            for q in range(parts):
                cols = slice(q * width, (q + 1) * width)
                nc.vector.quantize_mx(
                    out=w1_w[a, b][:, cols].bitcast(FP8X4),
                    scales=w1_s[a, b][:, cols],
                    in_=w1_bf[a, b][:, 4 * q * width : 4 * (q + 1) * width],
                )

        nc.vector.memset(tab_s[:].bitcast(I32), 0)
        nc.gpsimd.memset(w2_s[:].rearrange("p a n -> p (a n)").bitcast(I32), 0)
        nc.sync.dma_start(out=idx[:], in_=offs)
        nc.sync.dma_start(out=p1[:], in_=pos1)
        nc.sync.dma_start(out=p2[:], in_=pos2)
        for a in range(2):
            nc.scalar.dma_start(out=w2_w[a][:].bitcast(I32), in_=w2_words[a].bitcast(I32))
        for q in range(4):
            nc.scalar.dma_start(
                out=tab_s[32 * q : 32 * q + 8, :].bitcast(I32),
                in_=tab_scales[:, 4 * q : 4 * q + 4, :].bitcast(I32),
            )
        load_tab(0)
        load_w1(w1_raw[0, 0], 0, 0)
        load_tab(1)
        load_w1(w1_last[0], 1, 0)
        load_w1(w1_last[1], 1, HALF)
        for a in range(2):
            load_w1(w1_raw[a, 1], a, BANK)
        nc.sync.dma_start(
            out=base_t[:].rearrange("p (b t) -> p b t", t=4), in_=base.rearrange("(b p t) -> p b t", b=2, t=4)
        )
        nc.sync.dma_start(
            out=gain_t[:].rearrange("p (b t) -> p b t", t=4), in_=gain.rearrange("(b p t) -> p b t", b=2, t=4)
        )
        for q in range(4):
            nc.sync.dma_start(
                out=w2_s[32 * q : 32 * q + 4].bitcast(I32),
                in_=w2_scales[:, 4 * q : 4 * q + 4, :].rearrange("a r n -> r a n").bitcast(I32),
            )

        nc.vector.tensor_copy(out=v_w[0][:], in_=tab_w[0][:].indirect(idx[:]))
        nc.vector.tensor_copy(out=v_s[:], in_=tab_s[:].indirect(idx[:]))
        round_w1(0, 0, w1_raw[0, 0], 0, 0, 128, nc.scalar.copy)
        nc.vector.tensor_copy(out=v_w[1][:], in_=tab_w[1][:].indirect(idx[:]))
        quantize_w1(0, 0, 1)
        round_w1(1, 0, w1_last[0], 0, 0, 64, nc.scalar.copy)
        round_w1(1, 0, w1_last[1], 64, 64, 96, nc.scalar.copy)
        round_w1(1, 0, w1_last[1], 64, 96, 128, nc.vector.tensor_copy)
        quantize_w1(1, 0, 4)
        nc.gpsimd.tensor_scalar(out=base_share[:], in0=base_t[:], scalar1=1.0 / PL, scalar2=0.0, op0=ALU.mult, op1=ALU.add)

        h_rows, looked, neg_tops = {}, {}, {}
        tops_of = {}

        def first_stage(i):
            b, t = divmod(i, 4)
            m_cols = slice(P * t, P * (t + 1))
            h = ring.tile([P, S], F32, name="h")
            tops = ring.tile([P, 2], F32, name="tops")
            for half in range(2):
                cols = slice(BANK * half, BANK * (half + 1))
                acc = psum.tile([P, BANK], F32, name="acc", tag="bank%d" % ((2 * i + half) % 8))
                for a in range(2):
                    nc.tensor.matmul_mx(
                        out=acc[:],
                        lhsT=w1_w[a, b][:, m_cols].bitcast(FP8X4),
                        lhsT_scale=w1_s[a, b][:, m_cols],
                        rhs=v_w[a][:, cols].bitcast(FP8X4),
                        rhs_scale=v_s[4 * a :, cols],
                        start=(a == 0),
                        stop=(a == 1),
                    )
                nc.vector.tensor_scalar(
                    out=h[:, cols], in0=acc[:], scalar1=1.0, scalar2=None, op0=ALU.mult, op1=ALU.max,
                    accum_out=tops[:, half : half + 1],
                )
            h_rows[i], tops_of[i] = h, tops

        def negate_top(i):
            tops = tops_of[i]
            neg_top = ring.tile([P, 1], F32, name="neg_top")
            nc.vector.tensor_scalar(
                out=neg_top[:], in0=tops[:, 0:1], scalar1=tops[:, 1:2], scalar2=-1.0, op0=ALU.max, op1=ALU.mult
            )
            neg_tops[i] = neg_top

        def look(i):
            h, neg_top = h_rows[i], neg_tops[i]
            a_look = ring.tile([P, PL], F32, name="a_look")
            nc.scalar.activation(out=a_look[:], in_=h[:].indirect(p1[:]), func=ACT.Exp, bias=neg_top[:])
            looked[i] = a_look

        def row_sum(i):
            a_look = looked[i]
            shifted = ring.tile([P, PL], F32, name="shifted")
            nc.scalar.activation(
                out=shifted[:], in_=a_look[:], func=ACT.Identity, bias=base_share[:, i : i + 1], accum_out=den[i][:]
            )

        def pick(i, m0=0, m1=PL):
            nc.vector.tensor_tensor(
                out=prod[i][:, m0:m1], in0=h_rows[i][:].indirect(p2[:, m0 // 16 : m1 // 16]),
                in1=looked[i][:, m0:m1], op=ALU.mult,
            )

        def invert(i):
            inv = ring.tile([P, 1], F32, name="inv")
            nc.vector.reciprocal(out=inv[:], in_=den[i][:])
            return inv

        def times_gain(i, inv):
            factor = ring.tile([P, 1], F32, name="factor")
            nc.vector.tensor_tensor(out=factor[:], in0=inv[:], in1=gain_t[:, i : i + 1], op=ALU.mult)
            return factor

        def scale_rows(i, inv, engine, m0=0, m1=PL):
            b, t = divmod(i, 4)
            engine.tensor_scalar(
                out=z_rows[b][:, t, m0:m1], in0=prod[i][:, m0:m1], scalar1=inv[:], scalar2=gain_t[:, i : i + 1],
                op0=ALU.mult, op1=ALU.mult,
            )

        def scale_rows_on_scalar(i, factor):
            b, t = divmod(i, 4)
            nc.scalar.activation(out=z_rows[b][:, t, :], in_=prod[i][:], func=ACT.Copy, scale=factor[:])

        def weave_z(b, c, copy):
            src = z_rows[b][:, :, P * c : P * (c + 1)]
            copy(
                out=z_bf[b, c][:].rearrange("p (g i) t -> p g t i", i=4),
                in_=src.rearrange("p t (g i) -> p g t i", i=4),
            )

        def second_stage(b, c):
            nc.vector.quantize_mx(
                out=z_w[b, c][:].bitcast(FP8X4), scales=z_s[b, c][:], in_=z_bf[b, c][:].rearrange("p m t -> p (m t)")
            )
            if b == 0:
                y_bank[c] = psum.tile([P, BANK], F32, name="y", tag="bank%d" % c)
            for j in range(4):
                n0 = P * j
                nc.tensor.matmul_mx(
                    out=y_bank[c][:, n0 : n0 + P],
                    lhsT=w2_w[b][:, 2 * n0 : 2 * (n0 + P)].bitcast(FP4X4),
                    lhsT_scale=w2_s[:, b, n0 : n0 + P],
                    rhs=z_w[b, c][:].bitcast(FP8X4),
                    rhs_scale=z_s[b, c][:],
                    start=(b == 0 and j == 0),
                    stop=(b == 1 and j == 3),
                )

        first_stage(0)
        round_w1(0, 1, w1_raw[0, 1], 0, 0, 64, nc.scalar.copy)
        round_w1(0, 1, w1_raw[0, 1], 0, 64, 128, copy_on_gpsimd)
        first_stage(1)
        negate_top(0)
        look(0)
        round_w1(1, 1, w1_raw[1, 1], 0, 0, 40, copy_on_gpsimd)
        round_w1(1, 1, w1_raw[1, 1], 0, 40, 80, copy_on_gpsimd)
        round_w1(1, 1, w1_raw[1, 1], 0, 80, 128, nc.scalar.copy)
        row_sum(0)
        first_stage(2)
        negate_top(1)
        look(1)
        row_sum(1)
        first_stage(3)
        negate_top(2)
        look(2)
        row_sum(2)
        quantize_w1(0, 1, 1)
        negate_top(3)
        look(3)
        row_sum(3)
        inv = invert(0)
        quantize_w1(1, 1, 1)
        factor = times_gain(0, inv)
        pick(0)
        scale_rows_on_scalar(0, factor)
        inv = invert(1)
        pick(1)
        scale_rows(1, inv, nc.gpsimd)
        for i in range(2, 5):
            first_stage(i + 2)
            inv = invert(i)
            pick(i)
            scale_rows(i, inv, nc.gpsimd)
            negate_top(i + 2)
            if i == 4:
                weave_z(0, 0, nc.scalar.copy)
                weave_z(0, 1, nc.scalar.copy)
            look(i + 2)
            row_sum(i + 2)
        first_stage(7)
        inv = invert(5)
        negate_top(7)
        look(7)
        row_sum(7)
        factor = times_gain(5, inv)
        pick(5)
        scale_rows_on_scalar(5, factor)
        inv = invert(6)
        second_stage(0, 0)
        factor = times_gain(6, inv)
        pick(6)
        scale_rows_on_scalar(6, factor)
        weave_z(0, 2, nc.scalar.copy)
        weave_z(0, 3, nc.scalar.copy)
        second_stage(0, 1)
        inv = invert(7)
        pick(7, 0, HALF)
        pick(7, HALF, PL)
        scale_rows(7, inv, nc.vector, 0, HALF)
        scale_rows(7, inv, nc.vector, HALF, PL)
        weave_z(1, 0, nc.vector.tensor_copy)
        for c in range(4):
            if c + 1 < 4:
                weave_z(1, c + 1, nc.vector.tensor_copy)
            second_stage(1, c)
            if c in (0, 1):
                second_stage(0, c + 2)

        for c in range(4):
            nc.scalar.activation(out=exp_y[:, c, :], in_=y_bank[c][:], func=ACT.Exp)
        nc.vector.tensor_scalar(
            out=one_plus[:], in0=exp_y[:], scalar1=EXP_CAP, scalar2=1.0, op0=ALU.min, op1=ALU.add
        )
        pieces = [(0, 0, 2), (0, 2, 4), (1, 0, 4), (2, 0, 4), (3, 0, 2), (3, 2, 4)]
        for c, j0, j1 in pieces:
            cols = slice(P * j0, P * j1)
            log_t = keep.tile([P, P * (j1 - j0)], F32, name="log_t%d%d" % (c, j0))
            nc.scalar.activation(out=log_t[:], in_=one_plus[:, c, cols], func=ACT.Ln)
            res = keep.tile([P, j1 - j0, P], F32, name="res%d%d" % (c, j0))
            nc.vector.tensor_tensor(
                out=res[:].rearrange("p j m -> p (j m)"), in0=log_t[:], in1=y_bank[c][:, cols], op=ALU.max
            )
            rows = out[P * j0 : P * j1, P * c : P * (c + 1)]
            nc.sync.dma_start(out=rows.rearrange("(j p) m -> p j m", p=P), in_=res[:])
